import numpy as np
import ml_dtypes


def mxq(x, axis, fmt="e4m3"):
    dtype, down = {"e4m3": (ml_dtypes.float8_e4m3fn, 7), "e5m2": (ml_dtypes.float8_e5m2, 14)}[fmt]
    v = np.moveaxis(np.asarray(x, np.float32).astype(ml_dtypes.bfloat16).astype(np.float64), axis, -1)
    blocks = v.reshape(v.shape[:-1] + (-1, 32))
    amax = np.abs(blocks).max(-1, keepdims=True)
    byte = np.maximum(np.where(amax > 0, np.frexp(amax)[1] - 1 + 127, 0) - down, 1)
    scale = np.exp2(byte - 127.0)
    codes = (blocks / scale).astype(np.float32).astype(dtype).astype(np.float64)
    return np.moveaxis((codes * scale).reshape(v.shape), -1, axis)


WIDE = False


def mx_kscale(k):
    if not WIDE:
        return np.ones(k)
    levels = np.array([10, -10, 5, -5, 0])
    if k % 512:
        return np.exp2(np.random.permutation(np.resize(levels, k // 32))).repeat(32)
    a = np.empty((k // 512, 16))
    for p in range(k // 512):
        a[p, :8] = np.random.permutation(np.resize(levels, 8))
        for g in range(8):
            far = levels[np.abs(levels - a[p, g]) >= 10]
            a[p, g + 8] = far[np.random.randint(len(far))]
    return np.exp2(a.ravel()).repeat(32)


def f64(x):
    return np.asarray(x).astype(np.float64)


def striped(idx):
    return np.tile(idx.reshape(-1, 16).T, (8, 1)).astype(np.uint16)


def unstriped(offs):
    return offs[:16].T.reshape(-1).astype(np.int64)


def pack_weight(w):
    k, n = w.shape
    w = f64(np.asarray(w, np.float32).astype(ml_dtypes.bfloat16)).reshape(k // 32, 32, n)
    amax = np.abs(w).max(1)
    byte = np.clip(np.where(amax > 0, np.frexp(amax)[1] - 1 + 127 - 7, 1), 1, 254)
    scaled = (w * np.exp2(127.0 - byte)[:, None, :]).reshape(k, n).astype(np.float32)
    words = np.ascontiguousarray(scaled.reshape(k // 512, 128, 4, n).transpose(0, 1, 3, 2)).astype(ml_dtypes.float8_e4m3fn).view(np.uint8)
    return words, np.ascontiguousarray(byte.astype(np.uint8).reshape(k // 512, 16, n))


def unpack_weight(words, scales):
    g, p, n, _ = words.shape
    vals = np.ascontiguousarray(words).view(ml_dtypes.float8_e4m3fn).astype(np.float64) * np.repeat(np.exp2(scales.astype(np.float64) - 127.0), 8, axis=1)[..., None]
    return vals.transpose(0, 1, 3, 2).reshape(g * 512, n)


K, T, S, D, N, H = 512, 4096, 1024, 4, 256, 512


def setup_inputs():
    n = np.random.standard_normal
    s = mx_kscale(K)[:, None]
    u = mx_kscale(H)
    packed_xT = pack_weight(n((K, T)) * s)
    return {
        "x_words": packed_xT[0],
        "x_scales": packed_xT[1],
        "w1": (n((K, H)) / np.sqrt(K) / s).astype(np.float32),
        "w2": (n((K, H)) / np.sqrt(K) / s).astype(np.float32),
        "nu": (0.7 * n((H, S))).astype(np.float32),
        "obs": (np.random.uniform(0.1, 0.4, (H, S))).astype(np.float32),
        "unit": (np.random.uniform(0.6, 1.4, (H, 1)) * u[:, None]).astype(np.float32),
        "w3": (n((H, N)) / np.sqrt(H) / u[:, None]).astype(np.float32),
        "offs": striped(np.random.permutation(T)[:S]),
    }


def reference(x_words, x_scales, w1, w2, nu, obs, unit, w3, offs):
    xq = unpack_weight(x_words, x_scales)[:, unstriped(offs)]
    dl = mxq(f64(w1), 0, "e4m3").T @ xq
    mu = mxq(f64(w2), 0, "e4m3").T @ xq
    util = np.tanh(dl) + np.tanh(mu) * f64(nu)
    eu = np.exp(0.9 * util)
    mkt = eu.reshape(len(eu), -1, D).sum(axis=2)
    shr = eu / (np.repeat(mkt, D, axis=1) + 1.0)
    dnew = dl + np.log(f64(obs)) - np.log(shr)
    hid = f64(unit) * dnew
    return mxq(f64(w3), 0, "e4m3").T @ mxq(hid, 0, "e4m3")

@@ -1,0 +1,189 @@
+from contextlib import ExitStack
+
+import concourse.mybir as mybir
+from concourse.masks import make_identity
+
+K, T, S, D, N, H = 512, 4096, 1024, 4, 256, 512
+FLOPS = 2 * (2 * K * H * S + H * N * S)
+
+F32 = mybir.dt.float32
+BF16 = mybir.dt.bfloat16
+I32 = mybir.dt.int32
+U32 = mybir.dt.uint32
+U16 = mybir.dt.uint16
+U8 = mybir.dt.uint8
+FP8X4 = mybir.dt.float8_e4m3fn_x4
+ALU = mybir.AluOpType
+ACT = mybir.ActivationFunctionType
+
+P = 128
+PACK = 4
+HALF = 512
+HALVES = S // HALF
+MARKETS = HALF // D
+PIECE = 256
+TASTE = 0.9
+SMALLEST_NORMAL = 2.0 ** -126
+
+
+def tile_picked_yblpsh_inv_p_kernel(tc, x_words, x_scales, w1, w2, nu, obs, unit, w3, offs, out):
+    nc = tc.nc
+    with ExitStack() as ctx:
+        keep = ctx.enter_context(tc.tile_pool(name="keep", bufs=1))
+        ring = ctx.enter_context(tc.tile_pool(name="ring", bufs=3))
+        psum = ctx.enter_context(tc.psum_pool(name="psum", bufs=2))
+
+        offsets = keep.tile([P, S // 16], U16, name="offsets")
+        nc.sync.dma_start(offsets[:], offs)
+        unit_sb = keep.tile([P, PACK], F32, name="unit_sb")
+        nc.sync.dma_start(unit_sb[:], unit.rearrange("(p t) o -> p (t o)", t=PACK))
+
+        scale_table = keep.tile([P, T], U8, name="scale_table", align_bytes=64)
+        nc.vector.memset(scale_table[:].bitcast(I32), 0)
+        w2_raw = keep.tile([P, PACK, H], F32, name="w2_raw")
+        nc.sync.dma_start(w2_raw[:], w2.rearrange("(p j) c -> p j c", j=PACK))
+        for q in range(4):
+            nc.sync.dma_start(scale_table[32 * q : 32 * q + 4, :].bitcast(I32), x_scales[0, 4 * q : 4 * q + 4, :].bitcast(I32))
+        w1_raw = keep.tile([P, PACK, H], F32, name="w1_raw")
+        nc.sync.dma_start(w1_raw[:], w1.rearrange("(p j) c -> p j c", j=PACK))
+        word_table = keep.tile([P, T], I32, name="word_table", align_bytes=64)
+        nc.sync.dma_start(word_table[:], x_words[0].rearrange("p n t -> p (n t)").bitcast(I32))
+
+        nu_rows = nu.rearrange("(p t) j -> p t j", t=PACK)
+        obs_rows = obs.rearrange("(p t) j -> p t j", t=PACK)
+        nu_sb = {}
+        for h in range(HALVES):
+            for t in range(PACK):
+                nu_sb[h, t] = keep.tile([P, HALF], F32, name=f"nu_{h}_{t}")
+                nc.sync.dma_start(nu_sb[h, t][:], nu_rows[:, t, h * HALF : (h + 1) * HALF])
+        w3_raw = keep.tile([P, PACK, N], F32, name="w3_raw")
+        nc.sync.dma_start(w3_raw[:], w3.rearrange("(p j) c -> p j c", j=PACK))
+        obs_sb = {}
+        for h in range(HALVES):
+            obs_sb[h] = keep.tile([P, PACK, HALF], F32, name=f"obs_{h}")
+            nc.sync.dma_start(obs_sb[h][:], obs_rows[:, :, h * HALF : (h + 1) * HALF])
+
+        identity = keep.tile([P, P], F32, name="identity")
+        make_identity(nc, identity[:])
+
+        neg_unit = keep.tile([P, PACK], F32, name="neg_unit")
+        nc.vector.tensor_scalar(neg_unit[:], unit_sb[:], -1.0, None, ALU.mult)
+        taste_unit = keep.tile([P, PACK], F32, name="taste_unit")
+        nc.vector.tensor_scalar(taste_unit[:], unit_sb[:], -TASTE, None, ALU.mult)
+        abs_unit = keep.tile([P, PACK], F32, name="abs_unit")
+        nc.vector.tensor_tensor(abs_unit[:], unit_sb[:], neg_unit[:], ALU.max)
+        vanishes = keep.tile([P, PACK], F32, name="vanishes")
+        nc.vector.tensor_scalar(vanishes[:], abs_unit[:], SMALLEST_NORMAL, None, ALU.is_lt)
+        divisor = keep.tile([P, PACK], F32, name="divisor")
+        nc.vector.tensor_tensor(divisor[:], neg_unit[:], vanishes[:], ALU.subtract)
+        undo_unit = keep.tile([P, PACK], F32, name="undo_unit")
+        nc.vector.reciprocal(undo_unit[:], divisor[:])
+
+        def quantize(name, grouped, width):
+            codes = keep.tile([P, width], U32, name=name + "_codes", align_bytes=64)
+            scales = keep.tile([P, width], U8, name=name + "_scales", align_bytes=64)
+            nc.vector.quantize_mx(out=codes[:].bitcast(FP8X4), scales=scales[:], in_=grouped)
+            return codes, scales
+
+        def dealt_views(grouped, raw):
+            return (
+                grouped[:].rearrange("p (t m j) -> p m t j", t=PACK, j=PACK),
+                raw[:].rearrange("p j (m t) -> p m t j", t=PACK),
+            )
+
+        w2_grouped = keep.tile([P, PACK * H], BF16, name="w2_grouped", align_bytes=64)
+        nc.vector.tensor_copy(*dealt_views(w2_grouped, w2_raw))
+        w1_grouped = keep.tile([P, PACK * H], BF16, name="w1_grouped", align_bytes=64)
+        nc.scalar.copy(*dealt_views(w1_grouped, w1_raw))
+
+        x_scale = keep.tile([P, S], U8, name="x_scale", align_bytes=64)
+        nc.vector.tensor_copy(x_scale[:], scale_table[:].indirect(offsets[:]))
+        w2_codes, w2_scales = quantize("w2", w2_grouped[:], H)
+        w1_codes, w1_scales = quantize("w1", w1_grouped[:], H)
+
+        x_code = []
+        for h in range(HALVES):
+            picked = keep.tile([P, HALF], U32, name=f"x_code_{h}", align_bytes=64)
+            cols = slice(h * HALF // 16, (h + 1) * HALF // 16)
+            nc.vector.tensor_copy(picked[:], word_table[:].bitcast(U32).indirect(offsets[:, cols]))
+            x_code.append(picked)
+
+        def mx_product(acc, w_codes, w_scales, w_cols, codes, scales):
+            nc.tensor.matmul_mx(
+                out=acc,
+                lhsT=w_codes[:, w_cols].bitcast(FP8X4),
+                lhsT_scale=w_scales[:, w_cols],
+                rhs=codes.bitcast(FP8X4),
+                rhs_scale=scales,
+                start=True,
+                stop=True,
+            )
+
+        slots = HALVES * PACK + HALVES
+        pull = keep.tile([P, slots, HALF], F32, name="pull", tag="phase")
+        partial = keep.tile([P, HALVES * PACK, HALF], F32, name="partial")
+        market_sums = []
+        for h in range(HALVES):
+            goods = slice(h * HALF, (h + 1) * HALF)
+            market_sum = psum.tile([P, PACK, P], F32, name=f"market_sum_{h}", tag="market")
+            market_sums.append(market_sum)
+            for t in range(PACK):
+                c = h * PACK + t
+                w_cols = slice(t * P, (t + 1) * P)
+                mu = psum.tile([P, HALF], F32, name="mu", tag="mu")
+                mx_product(mu[:], w2_codes, w2_scales, w_cols, x_code[h][:], x_scale[:, goods])
+                dl = psum.tile([P, HALF], F32, name="dl", tag="dl", bufs=4)
+                mx_product(dl[:], w1_codes, w1_scales, w_cols, x_code[h][:], x_scale[:, goods])
+                tanh_mu = ring.tile([P, HALF], F32, name="tanh_mu")
+                nc.scalar.activation(tanh_mu[:], mu[:], ACT.Tanh)
+                tanh_dl = ring.tile([P, HALF], F32, name="tanh_dl")
+                nc.scalar.activation(tanh_dl[:], dl[:], ACT.Tanh)
+                taste = ring.tile([P, HALF], F32, name="taste")
+                nc.vector.scalar_tensor_tensor(taste[:], tanh_mu[:], taste_unit[:, t : t + 1], nu_sb[h, t][:], ALU.mult, ALU.mult)
+                nc.vector.scalar_tensor_tensor(pull[:, c, :], tanh_dl[:], taste_unit[:, t : t + 1], taste[:], ALU.mult, ALU.add)
+                eu = ring.tile([P, HALF], F32, name="eu")
+                nc.scalar.activation(eu[:], pull[:, c, :], ACT.Exp, scale=undo_unit[:, t : t + 1])
+                nc.vector.scalar_tensor_tensor(partial[:, c, :], dl[:], unit_sb[:, t : t + 1], pull[:, c, :], ALU.mult, ALU.add)
+                for d in range(D):
+                    nc.tensor.matmul(market_sum[:, t, :], eu[:, d::D], identity[:], start=(d == 0), stop=(d == D - 1), is_transpose=True)
+
+        w3_grouped = keep.tile([P, PACK * N], BF16, name="w3_grouped", align_bytes=64)
+        nc.vector.tensor_copy(
+            w3_grouped[:].rearrange("p (c i j) -> p c j i", i=4, j=PACK),
+            w3_raw[:].rearrange("p j (c i) -> p c j i", i=4),
+        )
+        w3_codes, w3_scales = quantize("w3", w3_grouped[:], N)
+
+        logs = keep.tile([P, slots, HALF], F32, name="logs", tag="phase")
+        out_rows = out.rearrange("(b m) j -> m b j", m=P)
+        for h in range(HALVES):
+            log_market_t = logs[:, HALVES * PACK + h, :]
+            nc.scalar.activation(log_market_t, market_sums[h][:].rearrange("v t p -> v (t p)"), ACT.Ln, bias=1.0)
+            turned = psum.tile([P, PACK, MARKETS], F32, name="turned", tag="mu")
+            for t in range(PACK):
+                nc.tensor.transpose(turned[:, t, :], log_market_t[:, t * P : (t + 1) * P], identity[:])
+            log_market = keep.tile([P, PACK, MARKETS], F32, name=f"log_market_{h}")
+            summed = keep.tile([P, PACK, HALF], F32, name=f"summed_{h}")
+            for t in range(PACK):
+                c = h * PACK + t
+                nc.scalar.activation(logs[:, c, :], obs_sb[h][:, t, :], ACT.Ln)
+                nc.vector.scalar_tensor_tensor(summed[:, t, :], logs[:, c, :], unit_sb[:, t : t + 1], partial[:, c, :], ALU.mult, ALU.add)
+            for t in range(PACK):
+                nc.scalar.activation(log_market[:, t, :], turned[:, t, :], ACT.Copy, scale=unit_sb[:, t : t + 1])
+            for s in range(HALF // PIECE):
+                markets = PIECE // D
+                hid = ring.tile([P, PIECE * PACK], BF16, name="hid", align_bytes=64)
+                nc.vector.tensor_tensor(
+                    hid[:].rearrange("p (v d t) -> p v t d", d=D, t=PACK),
+                    summed[:, :, s * PIECE : (s + 1) * PIECE].rearrange("p t (v d) -> p v t d", d=D),
+                    log_market[:, :, s * markets : (s + 1) * markets].rearrange("p t v -> p v t").unsqueeze(3).to_broadcast([P, markets, PACK, D]),
+                    ALU.add,
+                )
+                hid_codes, hid_scales = quantize(f"hid_{h}_{s}", hid[:], PIECE)
+                acc = psum.tile([P, N // P, PIECE], F32, name="acc", tag="dl", bufs=4)
+                for b in range(N // P):
+                    mx_product(acc[:, b, :], w3_codes, w3_scales, slice(b * P, (b + 1) * P), hid_codes[:], hid_scales[:])
+                result = ring.tile([P, N // P, PIECE], F32, name="result")
+                nc.scalar.copy(result[:], acc[:])
+                j0 = h * HALF + s * PIECE
+                nc.sync.dma_start(out_rows[:, :, j0 : j0 + PIECE], result[:])

@@ -18,12 +18,19 @@ ACT = mybir.ActivationFunctionType
 
 P = 128
 PACK = 4
+QUADRANTS = 4
+LIST_ROWS = 16
 HALF = 512
 HALVES = S // HALF
+CHUNKS = HALVES * PACK
 MARKETS = HALF // D
-PIECE = 256
 TASTE = 0.9
 SMALLEST_NORMAL = 2.0 ** -126
+
+BANKS = 6
+LEAD = 4
+LAG = 4
+PIECES = ((256, 256), (256, 128, 128))
 
 
 def tile_picked_yblpsh_inv_p_kernel(tc, x_words, x_scales, w1, w2, nu, obs, unit, w3, offs, out):
@@ -31,23 +38,27 @@ def tile_picked_yblpsh_inv_p_kernel(tc, x_words, x_scales, w1, w2, nu, obs, unit
     with ExitStack() as ctx:
         keep = ctx.enter_context(tc.tile_pool(name="keep", bufs=1))
         ring = ctx.enter_context(tc.tile_pool(name="ring", bufs=3))
-        psum = ctx.enter_context(tc.psum_pool(name="psum", bufs=2))
+        psum = ctx.enter_context(tc.psum_pool(name="psum", bufs=HALVES))
 
-        offsets = keep.tile([P, S // 16], U16, name="offsets")
-        nc.sync.dma_start(offsets[:], offs)
         unit_sb = keep.tile([P, PACK], F32, name="unit_sb")
         nc.sync.dma_start(unit_sb[:], unit.rearrange("(p t) o -> p (t o)", t=PACK))
+        offsets = keep.tile([P, S // LIST_ROWS], U16, name="offsets")
+        nc.sync.dma_start(offsets[:], offs)
 
+        scale_rows = keep.tile([P, T // 4], I32, name="scale_rows")
+        for q in range(QUADRANTS):
+            nc.sync.dma_start(scale_rows[32 * q : 32 * q + 4, :], x_scales[0, 4 * q : 4 * q + 4, :].bitcast(I32))
         scale_table = keep.tile([P, T], U8, name="scale_table", align_bytes=64)
         nc.vector.memset(scale_table[:].bitcast(I32), 0)
-        w2_raw = keep.tile([P, PACK, H], F32, name="w2_raw")
+        for q in range(QUADRANTS):
+            nc.vector.tensor_copy(scale_table[32 * q : 32 * q + 4, :].bitcast(I32), scale_rows[32 * q : 32 * q + 4, :])
+
+        w2_raw = keep.tile([P, PACK, H], F32, name="w2_raw", tag="wide_0")
         nc.sync.dma_start(w2_raw[:], w2.rearrange("(p j) c -> p j c", j=PACK))
-        for q in range(4):
-            nc.sync.dma_start(scale_table[32 * q : 32 * q + 4, :].bitcast(I32), x_scales[0, 4 * q : 4 * q + 4, :].bitcast(I32))
-        w1_raw = keep.tile([P, PACK, H], F32, name="w1_raw")
-        nc.sync.dma_start(w1_raw[:], w1.rearrange("(p j) c -> p j c", j=PACK))
         word_table = keep.tile([P, T], I32, name="word_table", align_bytes=64)
         nc.sync.dma_start(word_table[:], x_words[0].rearrange("p n t -> p (n t)").bitcast(I32))
+        w1_raw = keep.tile([P, PACK, H], F32, name="w1_raw", tag="wide_1")
+        nc.sync.dma_start(w1_raw[:], w1.rearrange("(p j) c -> p j c", j=PACK))
 
         nu_rows = nu.rearrange("(p t) j -> p t j", t=PACK)
         obs_rows = obs.rearrange("(p t) j -> p t j", t=PACK)
@@ -66,17 +77,15 @@ def tile_picked_yblpsh_inv_p_kernel(tc, x_words, x_scales, w1, w2, nu, obs, unit
         identity = keep.tile([P, P], F32, name="identity")
         make_identity(nc, identity[:])
 
-        neg_unit = keep.tile([P, PACK], F32, name="neg_unit")
-        nc.vector.tensor_scalar(neg_unit[:], unit_sb[:], -1.0, None, ALU.mult)
         taste_unit = keep.tile([P, PACK], F32, name="taste_unit")
         nc.vector.tensor_scalar(taste_unit[:], unit_sb[:], -TASTE, None, ALU.mult)
         abs_unit = keep.tile([P, PACK], F32, name="abs_unit")
-        nc.vector.tensor_tensor(abs_unit[:], unit_sb[:], neg_unit[:], ALU.max)
+        nc.vector.scalar_tensor_tensor(abs_unit[:], unit_sb[:], -1.0, unit_sb[:], ALU.mult, ALU.max)
         vanishes = keep.tile([P, PACK], F32, name="vanishes")
         nc.vector.tensor_scalar(vanishes[:], abs_unit[:], SMALLEST_NORMAL, None, ALU.is_lt)
         divisor = keep.tile([P, PACK], F32, name="divisor")
-        nc.vector.tensor_tensor(divisor[:], neg_unit[:], vanishes[:], ALU.subtract)
-        undo_unit = keep.tile([P, PACK], F32, name="undo_unit")
+        nc.vector.scalar_tensor_tensor(divisor[:], unit_sb[:], -1.0, vanishes[:], ALU.mult, ALU.subtract)
+        undo_unit = keep.tile([P, PACK], F32, name="undo_unit", tag="phase")
         nc.vector.reciprocal(undo_unit[:], divisor[:])
 
         def quantize(name, grouped, width):
@@ -92,21 +101,21 @@ def tile_picked_yblpsh_inv_p_kernel(tc, x_words, x_scales, w1, w2, nu, obs, unit
             )
 
         w2_grouped = keep.tile([P, PACK * H], BF16, name="w2_grouped", align_bytes=64)
-        nc.vector.tensor_copy(*dealt_views(w2_grouped, w2_raw))
-        w1_grouped = keep.tile([P, PACK * H], BF16, name="w1_grouped", align_bytes=64)
-        nc.scalar.copy(*dealt_views(w1_grouped, w1_raw))
+        nc.scalar.copy(*dealt_views(w2_grouped, w2_raw))
 
         x_scale = keep.tile([P, S], U8, name="x_scale", align_bytes=64)
         nc.vector.tensor_copy(x_scale[:], scale_table[:].indirect(offsets[:]))
         w2_codes, w2_scales = quantize("w2", w2_grouped[:], H)
-        w1_codes, w1_scales = quantize("w1", w1_grouped[:], H)
 
         x_code = []
         for h in range(HALVES):
             picked = keep.tile([P, HALF], U32, name=f"x_code_{h}", align_bytes=64)
-            cols = slice(h * HALF // 16, (h + 1) * HALF // 16)
-            nc.vector.tensor_copy(picked[:], word_table[:].bitcast(U32).indirect(offsets[:, cols]))
+            entries = slice(h * HALF // LIST_ROWS, (h + 1) * HALF // LIST_ROWS)
+            nc.vector.tensor_copy(picked[:], word_table[:].bitcast(U32).indirect(offsets[:, entries]))
             x_code.append(picked)
+        w1_grouped = keep.tile([P, PACK * H], BF16, name="w1_grouped", align_bytes=64)
+        nc.vector.tensor_copy(*dealt_views(w1_grouped, w1_raw))
+        w1_codes, w1_scales = quantize("w1", w1_grouped[:], H)
 
         def mx_product(acc, w_codes, w_scales, w_cols, codes, scales):
             nc.tensor.matmul_mx(
@@ -119,71 +128,125 @@ def tile_picked_yblpsh_inv_p_kernel(tc, x_words, x_scales, w1, w2, nu, obs, unit
                 stop=True,
             )
 
-        slots = HALVES * PACK + HALVES
-        pull = keep.tile([P, slots, HALF], F32, name="pull", tag="phase")
-        partial = keep.tile([P, HALVES * PACK, HALF], F32, name="partial")
-        market_sums = []
-        for h in range(HALVES):
-            goods = slice(h * HALF, (h + 1) * HALF)
-            market_sum = psum.tile([P, PACK, P], F32, name=f"market_sum_{h}", tag="market")
-            market_sums.append(market_sum)
-            for t in range(PACK):
-                c = h * PACK + t
-                w_cols = slice(t * P, (t + 1) * P)
-                mu = psum.tile([P, HALF], F32, name="mu", tag="mu")
-                mx_product(mu[:], w2_codes, w2_scales, w_cols, x_code[h][:], x_scale[:, goods])
-                dl = psum.tile([P, HALF], F32, name="dl", tag="dl", bufs=4)
-                mx_product(dl[:], w1_codes, w1_scales, w_cols, x_code[h][:], x_scale[:, goods])
-                tanh_mu = ring.tile([P, HALF], F32, name="tanh_mu")
-                nc.scalar.activation(tanh_mu[:], mu[:], ACT.Tanh)
-                tanh_dl = ring.tile([P, HALF], F32, name="tanh_dl")
-                nc.scalar.activation(tanh_dl[:], dl[:], ACT.Tanh)
-                taste = ring.tile([P, HALF], F32, name="taste")
-                nc.vector.scalar_tensor_tensor(taste[:], tanh_mu[:], taste_unit[:, t : t + 1], nu_sb[h, t][:], ALU.mult, ALU.mult)
-                nc.vector.scalar_tensor_tensor(pull[:, c, :], tanh_dl[:], taste_unit[:, t : t + 1], taste[:], ALU.mult, ALU.add)
-                eu = ring.tile([P, HALF], F32, name="eu")
-                nc.scalar.activation(eu[:], pull[:, c, :], ACT.Exp, scale=undo_unit[:, t : t + 1])
-                nc.vector.scalar_tensor_tensor(partial[:, c, :], dl[:], unit_sb[:, t : t + 1], pull[:, c, :], ALU.mult, ALU.add)
-                for d in range(D):
-                    nc.tensor.matmul(market_sum[:, t, :], eu[:, d::D], identity[:], start=(d == 0), stop=(d == D - 1), is_transpose=True)
+        tanh_dl = keep.tile([P, CHUNKS, HALF], F32, name="tanh_dl", tag="late", align_bytes=64)
+        pull = keep.tile([P, CHUNKS, HALF], F32, name="pull")
+        partial = keep.tile([P, CHUNKS, HALF], F32, name="partial")
+        market_sums = [psum.tile([P, PACK, P], F32, name=f"market_sum_{h}", tag="market") for h in range(HALVES)]
+        dl_of = {}
+        tanh_mu = keep.tile([P, CHUNKS, HALF], F32, name="tanh_mu")
+        taste = keep.tile([P, CHUNKS, HALF], F32, name="taste")
 
-        w3_grouped = keep.tile([P, PACK * N], BF16, name="w3_grouped", align_bytes=64)
+        def product(c, w_codes, w_scales, tanh_to):
+            h, t = divmod(c, PACK)
+            acc = psum.tile([P, HALF], F32, name="acc", tag="bank", bufs=BANKS)
+            mx_product(acc[:], w_codes, w_scales, slice(t * P, (t + 1) * P), x_code[h][:], x_scale[:, h * HALF : (h + 1) * HALF])
+            nc.scalar.activation(tanh_to[:, c, :], acc[:], ACT.Tanh)
+            return acc
+
+        def weigh_taste(c):
+            h, t = divmod(c, PACK)
+            nc.vector.scalar_tensor_tensor(taste[:, c, :], tanh_mu[:, c, :], taste_unit[:, t : t + 1], nu_sb[h, t][:], ALU.mult, ALU.mult)
+
+        def shares(c):
+            h, t = divmod(c, PACK)
+            nc.vector.scalar_tensor_tensor(pull[:, c, :], tanh_dl[:, c, :], taste_unit[:, t : t + 1], taste[:, c, :], ALU.mult, ALU.add)
+            eu = ring.tile([P, 2, MARKETS, 2], F32, name="eu")
+            nc.scalar.activation(
+                eu[:].rearrange("p e v d -> p v e d"),
+                pull[:, c, :].rearrange("p (v e d) -> p v e d", e=2, d=2),
+                ACT.Exp,
+                scale=undo_unit[:, t : t + 1],
+            )
+            for good in range(D):
+                nc.tensor.matmul(
+                    market_sums[h][:, t, :],
+                    eu[:, good // 2, :, good % 2],
+                    identity[:],
+                    start=(good == 0),
+                    stop=(good == D - 1),
+                    is_transpose=True,
+                )
+
+        def add_mean_utility(c):
+            t = c % PACK
+            nc.vector.scalar_tensor_tensor(partial[:, c, :], dl_of[c][:], unit_sb[:, t : t + 1], pull[:, c, :], ALU.mult, ALU.add)
+
+        for c in range(CHUNKS):
+            product(c, w2_codes, w2_scales, tanh_mu)
+        for c in range(LEAD):
+            weigh_taste(c)
+        dl_of[0] = product(0, w1_codes, w1_scales, tanh_dl)
+        for c in range(CHUNKS):
+            if c + 1 < CHUNKS:
+                dl_of[c + 1] = product(c + 1, w1_codes, w1_scales, tanh_dl)
+            shares(c)
+            if c + LEAD < CHUNKS:
+                weigh_taste(c + LEAD)
+            if LAG - 1 <= c < CHUNKS - 1:
+                add_mean_utility(c - (LAG - 1))
+        for c in range(CHUNKS - LAG, CHUNKS):
+            add_mean_utility(c)
+
+        w3_grouped = keep.tile([P, PACK * N], BF16, name="w3_grouped", tag="late", align_bytes=64)
         nc.vector.tensor_copy(
             w3_grouped[:].rearrange("p (c i j) -> p c j i", i=4, j=PACK),
             w3_raw[:].rearrange("p j (c i) -> p c j i", i=4),
         )
         w3_codes, w3_scales = quantize("w3", w3_grouped[:], N)
 
-        logs = keep.tile([P, slots, HALF], F32, name="logs", tag="phase")
+        logs = keep.tile([P, CHUNKS + HALVES, HALF], F32, name="logs", tag="phase")
         out_rows = out.rearrange("(b m) j -> m b j", m=P)
+        made = []
+
+        def instruments(hid, first, width):
+            hid_codes, hid_scales = quantize(f"hid_{first}", hid[:], width)
+            result_acc = psum.tile([P, N // P, width], F32, name="result_acc", tag="bank", bufs=BANKS)
+            for b in range(N // P):
+                mx_product(result_acc[:, b, :], w3_codes, w3_scales, slice(b * P, (b + 1) * P), hid_codes[:], hid_scales[:])
+            made.append((result_acc, first, width))
+
+        def store(result_acc, first, width):
+            result = ring.tile([P, N // P, width], F32, name="result")
+            if first + width == S:
+                nc.vector.tensor_copy(result[:], result_acc[:])
+            else:
+                nc.scalar.copy(result[:], result_acc[:])
+            nc.sync.dma_start(out_rows[:, :, first : first + width], result[:])
+
+        hid_pieces = []
         for h in range(HALVES):
-            log_market_t = logs[:, HALVES * PACK + h, :]
-            nc.scalar.activation(log_market_t, market_sums[h][:].rearrange("v t p -> v (t p)"), ACT.Ln, bias=1.0)
-            turned = psum.tile([P, PACK, MARKETS], F32, name="turned", tag="mu")
-            for t in range(PACK):
-                nc.tensor.transpose(turned[:, t, :], log_market_t[:, t * P : (t + 1) * P], identity[:])
-            log_market = keep.tile([P, PACK, MARKETS], F32, name=f"log_market_{h}")
-            summed = keep.tile([P, PACK, HALF], F32, name=f"summed_{h}")
-            for t in range(PACK):
+            summed = keep.tile([P, PACK, HALF], F32, name=f"summed_{h}", tag=f"wide_{h}")
+
+            def add_log_obs(t):
                 c = h * PACK + t
                 nc.scalar.activation(logs[:, c, :], obs_sb[h][:, t, :], ACT.Ln)
                 nc.vector.scalar_tensor_tensor(summed[:, t, :], logs[:, c, :], unit_sb[:, t : t + 1], partial[:, c, :], ALU.mult, ALU.add)
+
+            add_log_obs(0)
+            log_market_t = logs[:, CHUNKS + h, :]
+            nc.scalar.activation(log_market_t, market_sums[h][:].rearrange("v t p -> v (t p)"), ACT.Ln, bias=1.0)
+            turned = psum.tile([P, PACK, MARKETS], F32, name="turned", tag="bank", bufs=BANKS)
+            for t in range(PACK):
+                nc.tensor.transpose(turned[:, t, :], log_market_t[:, t * P : (t + 1) * P], identity[:])
+            for t in range(1, PACK):
+                add_log_obs(t)
+            log_market = keep.tile([P, PACK, MARKETS], F32, name=f"log_market_{h}")
             for t in range(PACK):
                 nc.scalar.activation(log_market[:, t, :], turned[:, t, :], ACT.Copy, scale=unit_sb[:, t : t + 1])
-            for s in range(HALF // PIECE):
-                markets = PIECE // D
-                hid = ring.tile([P, PIECE * PACK], BF16, name="hid", align_bytes=64)
+            start = 0
+            for width in PIECES[h]:
+                markets = width // D
+                hid = ring.tile([P, width * PACK], BF16, name="hid", align_bytes=64)
                 nc.vector.tensor_tensor(
                     hid[:].rearrange("p (v d t) -> p v t d", d=D, t=PACK),
-                    summed[:, :, s * PIECE : (s + 1) * PIECE].rearrange("p t (v d) -> p v t d", d=D),
-                    log_market[:, :, s * markets : (s + 1) * markets].rearrange("p t v -> p v t").unsqueeze(3).to_broadcast([P, markets, PACK, D]),
+                    summed[:, :, start : start + width].rearrange("p t (v d) -> p v t d", d=D),
+                    log_market[:, :, start // D : start // D + markets].rearrange("p t v -> p v t").unsqueeze(3).to_broadcast([P, markets, PACK, D]),
                     ALU.add,
                 )
-                hid_codes, hid_scales = quantize(f"hid_{h}_{s}", hid[:], PIECE)
-                acc = psum.tile([P, N // P, PIECE], F32, name="acc", tag="dl", bufs=4)
-                for b in range(N // P):
-                    mx_product(acc[:, b, :], w3_codes, w3_scales, slice(b * P, (b + 1) * P), hid_codes[:], hid_scales[:])
-                result = ring.tile([P, N // P, PIECE], F32, name="result")
-                nc.scalar.copy(result[:], acc[:])
-                j0 = h * HALF + s * PIECE
-                nc.sync.dma_start(out_rows[:, :, j0 : j0 + PIECE], result[:])
+                hid_pieces.append((hid, h * HALF + start, width))
+                if len(hid_pieces) > 1:
+                    instruments(*hid_pieces[-2])
+                start = start + width
+        instruments(*hid_pieces[-1])
+        for piece in made:
+            store(*piece)

from contextlib import ExitStack

import concourse.mybir as mybir
from concourse.masks import make_identity

K, T, S, D, N, H = 512, 4096, 1024, 4, 256, 512
FLOPS = 2 * (2 * K * H * S + H * N * S)

F32 = mybir.dt.float32
BF16 = mybir.dt.bfloat16
I32 = mybir.dt.int32
U32 = mybir.dt.uint32
U16 = mybir.dt.uint16
U8 = mybir.dt.uint8
FP8X4 = mybir.dt.float8_e4m3fn_x4
ALU = mybir.AluOpType
ACT = mybir.ActivationFunctionType

P = 128
PACK = 4
QUADRANTS = 4
LIST_ROWS = 16
HALF = 512
HALVES = S // HALF
CHUNKS = HALVES * PACK
MARKETS = HALF // D
TASTE = 0.9
SMALLEST_NORMAL = 2.0 ** -126

BANKS = 6
LEAD = 4
LAG = 4
PIECES = ((256, 256), (256, 128, 128))


def tile_picked_yblpsh_inv_p_kernel(tc, x_words, x_scales, w1, w2, nu, obs, unit, w3, offs, out):
    nc = tc.nc
    with ExitStack() as ctx:
        keep = ctx.enter_context(tc.tile_pool(name="keep", bufs=1))
        ring = ctx.enter_context(tc.tile_pool(name="ring", bufs=3))
        psum = ctx.enter_context(tc.psum_pool(name="psum", bufs=HALVES))

        unit_sb = keep.tile([P, PACK], F32, name="unit_sb")
        nc.sync.dma_start(unit_sb[:], unit.rearrange("(p t) o -> p (t o)", t=PACK))
        offsets = keep.tile([P, S // LIST_ROWS], U16, name="offsets")
        nc.sync.dma_start(offsets[:], offs)

        scale_rows = keep.tile([P, T // 4], I32, name="scale_rows")
        for q in range(QUADRANTS):
            nc.sync.dma_start(scale_rows[32 * q : 32 * q + 4, :], x_scales[0, 4 * q : 4 * q + 4, :].bitcast(I32))
        scale_table = keep.tile([P, T], U8, name="scale_table", align_bytes=64)
        nc.vector.memset(scale_table[:].bitcast(I32), 0)
        for q in range(QUADRANTS):
            nc.vector.tensor_copy(scale_table[32 * q : 32 * q + 4, :].bitcast(I32), scale_rows[32 * q : 32 * q + 4, :])

        w2_raw = keep.tile([P, PACK, H], F32, name="w2_raw", tag="wide_0")
        nc.sync.dma_start(w2_raw[:], w2.rearrange("(p j) c -> p j c", j=PACK))
        word_table = keep.tile([P, T], I32, name="word_table", align_bytes=64)
        nc.sync.dma_start(word_table[:], x_words[0].rearrange("p n t -> p (n t)").bitcast(I32))
        w1_raw = keep.tile([P, PACK, H], F32, name="w1_raw", tag="wide_1")
        nc.sync.dma_start(w1_raw[:], w1.rearrange("(p j) c -> p j c", j=PACK))

        nu_rows = nu.rearrange("(p t) j -> p t j", t=PACK)
        obs_rows = obs.rearrange("(p t) j -> p t j", t=PACK)
        nu_sb = {}
        for h in range(HALVES):
            for t in range(PACK):
                nu_sb[h, t] = keep.tile([P, HALF], F32, name=f"nu_{h}_{t}")
                nc.sync.dma_start(nu_sb[h, t][:], nu_rows[:, t, h * HALF : (h + 1) * HALF])
        w3_raw = keep.tile([P, PACK, N], F32, name="w3_raw")
        nc.sync.dma_start(w3_raw[:], w3.rearrange("(p j) c -> p j c", j=PACK))
        obs_sb = {}
        for h in range(HALVES):
            obs_sb[h] = keep.tile([P, PACK, HALF], F32, name=f"obs_{h}")
            nc.sync.dma_start(obs_sb[h][:], obs_rows[:, :, h * HALF : (h + 1) * HALF])

        identity = keep.tile([P, P], F32, name="identity")
        make_identity(nc, identity[:])

        taste_unit = keep.tile([P, PACK], F32, name="taste_unit")
        nc.vector.tensor_scalar(taste_unit[:], unit_sb[:], -TASTE, None, ALU.mult)
        abs_unit = keep.tile([P, PACK], F32, name="abs_unit")
        nc.vector.scalar_tensor_tensor(abs_unit[:], unit_sb[:], -1.0, unit_sb[:], ALU.mult, ALU.max)
        vanishes = keep.tile([P, PACK], F32, name="vanishes")
        nc.vector.tensor_scalar(vanishes[:], abs_unit[:], SMALLEST_NORMAL, None, ALU.is_lt)
        divisor = keep.tile([P, PACK], F32, name="divisor")
        nc.vector.scalar_tensor_tensor(divisor[:], unit_sb[:], -1.0, vanishes[:], ALU.mult, ALU.subtract)
        undo_unit = keep.tile([P, PACK], F32, name="undo_unit", tag="phase")
        nc.vector.reciprocal(undo_unit[:], divisor[:])

        def quantize(name, grouped, width):
            codes = keep.tile([P, width], U32, name=name + "_codes", align_bytes=64)
            scales = keep.tile([P, width], U8, name=name + "_scales", align_bytes=64)
            nc.vector.quantize_mx(out=codes[:].bitcast(FP8X4), scales=scales[:], in_=grouped)
            return codes, scales

        def dealt_views(grouped, raw):
            return (
                grouped[:].rearrange("p (t m j) -> p m t j", t=PACK, j=PACK),
                raw[:].rearrange("p j (m t) -> p m t j", t=PACK),
            )

        w2_grouped = keep.tile([P, PACK * H], BF16, name="w2_grouped", align_bytes=64)
        nc.scalar.copy(*dealt_views(w2_grouped, w2_raw))

        x_scale = keep.tile([P, S], U8, name="x_scale", align_bytes=64)
        nc.vector.tensor_copy(x_scale[:], scale_table[:].indirect(offsets[:]))
        w2_codes, w2_scales = quantize("w2", w2_grouped[:], H)

        x_code = []
        for h in range(HALVES):
            picked = keep.tile([P, HALF], U32, name=f"x_code_{h}", align_bytes=64)
            entries = slice(h * HALF // LIST_ROWS, (h + 1) * HALF // LIST_ROWS)
            nc.vector.tensor_copy(picked[:], word_table[:].bitcast(U32).indirect(offsets[:, entries]))
            x_code.append(picked)
        w1_grouped = keep.tile([P, PACK * H], BF16, name="w1_grouped", align_bytes=64)
        nc.vector.tensor_copy(*dealt_views(w1_grouped, w1_raw))
        w1_codes, w1_scales = quantize("w1", w1_grouped[:], H)

        def mx_product(acc, w_codes, w_scales, w_cols, codes, scales):
            nc.tensor.matmul_mx(
                out=acc,
                lhsT=w_codes[:, w_cols].bitcast(FP8X4),
                lhsT_scale=w_scales[:, w_cols],
                rhs=codes.bitcast(FP8X4),
                rhs_scale=scales,
                start=True,
                stop=True,
            )

        tanh_dl = keep.tile([P, CHUNKS, HALF], F32, name="tanh_dl", tag="late", align_bytes=64)
        pull = keep.tile([P, CHUNKS, HALF], F32, name="pull")
        partial = keep.tile([P, CHUNKS, HALF], F32, name="partial")
        market_sums = [psum.tile([P, PACK, P], F32, name=f"market_sum_{h}", tag="market") for h in range(HALVES)]
        dl_of = {}
        tanh_mu = keep.tile([P, CHUNKS, HALF], F32, name="tanh_mu")
        taste = keep.tile([P, CHUNKS, HALF], F32, name="taste")

        def product(c, w_codes, w_scales, tanh_to):
            h, t = divmod(c, PACK)
            acc = psum.tile([P, HALF], F32, name="acc", tag="bank", bufs=BANKS)
            mx_product(acc[:], w_codes, w_scales, slice(t * P, (t + 1) * P), x_code[h][:], x_scale[:, h * HALF : (h + 1) * HALF])
            nc.scalar.activation(tanh_to[:, c, :], acc[:], ACT.Tanh)
            return acc

        def weigh_taste(c):
            h, t = divmod(c, PACK)
            nc.vector.scalar_tensor_tensor(taste[:, c, :], tanh_mu[:, c, :], taste_unit[:, t : t + 1], nu_sb[h, t][:], ALU.mult, ALU.mult)

        def shares(c):
            h, t = divmod(c, PACK)
            nc.vector.scalar_tensor_tensor(pull[:, c, :], tanh_dl[:, c, :], taste_unit[:, t : t + 1], taste[:, c, :], ALU.mult, ALU.add)
            eu = ring.tile([P, 2, MARKETS, 2], F32, name="eu")
            nc.scalar.activation(
                eu[:].rearrange("p e v d -> p v e d"),
                pull[:, c, :].rearrange("p (v e d) -> p v e d", e=2, d=2),
                ACT.Exp,
                scale=undo_unit[:, t : t + 1],
            )
            for good in range(D):
                nc.tensor.matmul(
                    market_sums[h][:, t, :],
                    eu[:, good // 2, :, good % 2],
                    identity[:],
                    start=(good == 0),
                    stop=(good == D - 1),
                    is_transpose=True,
                )

        def add_mean_utility(c):
            t = c % PACK
            nc.vector.scalar_tensor_tensor(partial[:, c, :], dl_of[c][:], unit_sb[:, t : t + 1], pull[:, c, :], ALU.mult, ALU.add)

        for c in range(CHUNKS):
            product(c, w2_codes, w2_scales, tanh_mu)
        for c in range(LEAD):
            weigh_taste(c)
        dl_of[0] = product(0, w1_codes, w1_scales, tanh_dl)
        for c in range(CHUNKS):
            if c + 1 < CHUNKS:
                dl_of[c + 1] = product(c + 1, w1_codes, w1_scales, tanh_dl)
            shares(c)
            if c + LEAD < CHUNKS:
                weigh_taste(c + LEAD)
            if LAG - 1 <= c < CHUNKS - 1:
                add_mean_utility(c - (LAG - 1))
        for c in range(CHUNKS - LAG, CHUNKS):
            add_mean_utility(c)

        w3_grouped = keep.tile([P, PACK * N], BF16, name="w3_grouped", tag="late", align_bytes=64)
        nc.vector.tensor_copy(
            w3_grouped[:].rearrange("p (c i j) -> p c j i", i=4, j=PACK),
            w3_raw[:].rearrange("p j (c i) -> p c j i", i=4),
        )
        w3_codes, w3_scales = quantize("w3", w3_grouped[:], N)

        logs = keep.tile([P, CHUNKS + HALVES, HALF], F32, name="logs", tag="phase")
        out_rows = out.rearrange("(b m) j -> m b j", m=P)
        made = []

        def instruments(hid, first, width):
            hid_codes, hid_scales = quantize(f"hid_{first}", hid[:], width)
            result_acc = psum.tile([P, N // P, width], F32, name="result_acc", tag="bank", bufs=BANKS)
            for b in range(N // P):
                mx_product(result_acc[:, b, :], w3_codes, w3_scales, slice(b * P, (b + 1) * P), hid_codes[:], hid_scales[:])
            made.append((result_acc, first, width))

        def store(result_acc, first, width):
            result = ring.tile([P, N // P, width], F32, name="result")
            if first + width == S:
                nc.vector.tensor_copy(result[:], result_acc[:])
            else:
                nc.scalar.copy(result[:], result_acc[:])
            nc.sync.dma_start(out_rows[:, :, first : first + width], result[:])

        hid_pieces = []
        for h in range(HALVES):
            summed = keep.tile([P, PACK, HALF], F32, name=f"summed_{h}", tag=f"wide_{h}")

            def add_log_obs(t):
                c = h * PACK + t
                nc.scalar.activation(logs[:, c, :], obs_sb[h][:, t, :], ACT.Ln)
                nc.vector.scalar_tensor_tensor(summed[:, t, :], logs[:, c, :], unit_sb[:, t : t + 1], partial[:, c, :], ALU.mult, ALU.add)

            add_log_obs(0)
            log_market_t = logs[:, CHUNKS + h, :]
            nc.scalar.activation(log_market_t, market_sums[h][:].rearrange("v t p -> v (t p)"), ACT.Ln, bias=1.0)
            turned = psum.tile([P, PACK, MARKETS], F32, name="turned", tag="bank", bufs=BANKS)
            for t in range(PACK):
                nc.tensor.transpose(turned[:, t, :], log_market_t[:, t * P : (t + 1) * P], identity[:])
            for t in range(1, PACK):
                add_log_obs(t)
            log_market = keep.tile([P, PACK, MARKETS], F32, name=f"log_market_{h}")
            for t in range(PACK):
                nc.scalar.activation(log_market[:, t, :], turned[:, t, :], ACT.Copy, scale=unit_sb[:, t : t + 1])
            start = 0
            for width in PIECES[h]:
                markets = width // D
                hid = ring.tile([P, width * PACK], BF16, name="hid", align_bytes=64)
                nc.vector.tensor_tensor(
                    hid[:].rearrange("p (v d t) -> p v t d", d=D, t=PACK),
                    summed[:, :, start : start + width].rearrange("p t (v d) -> p v t d", d=D),
                    log_market[:, :, start // D : start // D + markets].rearrange("p t v -> p v t").unsqueeze(3).to_broadcast([P, markets, PACK, D]),
                    ALU.add,
                )
                hid_pieces.append((hid, h * HALF + start, width))
                if len(hid_pieces) > 1:
                    instruments(*hid_pieces[-2])
                start = start + width
        instruments(*hid_pieces[-1])
        for piece in made:
            store(*piece)
